import numpy as np
import ml_dtypes


def mxq(x, axis, fmt="e4m3"):
    dtype, down = {"e4m3": (ml_dtypes.float8_e4m3fn, 7), "e5m2": (ml_dtypes.float8_e5m2, 14)}[fmt]
    v = np.moveaxis(np.asarray(x, np.float32).astype(ml_dtypes.bfloat16).astype(np.float64), axis, -1)
    blocks = v.reshape(v.shape[:-1] + (-1, 32))
    amax = np.abs(blocks).max(-1, keepdims=True)
    byte = np.maximum(np.where(amax > 0, np.frexp(amax)[1] - 1 + 127, 0) - down, 1)
    scale = np.exp2(byte - 127.0)
    codes = (blocks / scale).astype(np.float32).astype(dtype).astype(np.float64)
    return np.moveaxis((codes * scale).reshape(v.shape), -1, axis)


WIDE = False


def mx_kscale(k):
    if not WIDE:
        return np.ones(k)
    levels = np.array([10, -10, 5, -5, 0])
    if k % 512:
        return np.exp2(np.random.permutation(np.resize(levels, k // 32))).repeat(32)
    a = np.empty((k // 512, 16))
    for p in range(k // 512):
        a[p, :8] = np.random.permutation(np.resize(levels, 8))
        for g in range(8):
            far = levels[np.abs(levels - a[p, g]) >= 10]
            a[p, g + 8] = far[np.random.randint(len(far))]
    return np.exp2(a.ravel()).repeat(32)


def f64(x):
    return np.asarray(x).astype(np.float64)


def striped(idx):
    return np.tile(idx.reshape(-1, 16).T, (8, 1)).astype(np.uint16)


def unstriped(offs):
    return offs[:16].T.reshape(-1).astype(np.int64)


E2M1 = np.array([0.0, 0.5, 1.0, 1.5, 2.0, 3.0, 4.0, 6.0, -0.0, -0.5, -1.0, -1.5, -2.0, -3.0, -4.0, -6.0])


def pack_weight(w, fmt):
    k, n = w.shape
    w = f64(np.asarray(w, np.float32).astype(ml_dtypes.bfloat16)).reshape(k // 32, 32, n)
    amax = np.abs(w).max(1)
    if fmt == "e4m3":
        byte = np.frexp(amax)[1] - 1 + 127 - 7
    else:
        mant, ex = np.frexp(amax / 6.0)
        byte = np.where(mant > 0.5, ex, ex - 1) + 127
    byte = np.clip(np.where(amax > 0, byte, 1), 1, 254)
    scaled = (w * np.exp2(127.0 - byte)[:, None, :]).reshape(k, n).astype(np.float32)
    by_word = np.ascontiguousarray(scaled.reshape(k // 512, 128, 4, n).transpose(0, 1, 3, 2))
    if fmt == "e4m3":
        words = by_word.astype(ml_dtypes.float8_e4m3fn).view(np.uint8)
    else:
        c = by_word.astype(ml_dtypes.float4_e2m1fn).view(np.uint8) & 0xF
        words = (c[..., 0::2] | (c[..., 1::2] << 4)).reshape(k // 512, 128, 2 * n)
    return np.ascontiguousarray(words), np.ascontiguousarray(byte.astype(np.uint8).reshape(k // 512, 16, n))


def unpack_weight(words, scales, fmt):
    g, _, n = scales.shape
    words = np.ascontiguousarray(words).reshape(g, 128, n, -1)
    if fmt == "e4m3":
        vals = words.view(ml_dtypes.float8_e4m3fn).astype(np.float64)
    else:
        nib = np.empty((g, 128, n, 4), np.uint8)
        nib[..., 0::2] = words & 0xF
        nib[..., 1::2] = words >> 4
        vals = E2M1[nib]
    vals = vals * np.repeat(np.exp2(scales.astype(np.float64) - 127.0), 8, axis=1)[..., None]
    return vals.transpose(0, 1, 3, 2).reshape(g * 512, n)


def gelu(v):
    return 0.5 * v * (1.0 + np.tanh(np.sqrt(2.0 / np.pi) * (v + 0.044715 * v**3)))


K, H, N, T, S, T2, P = 1024, 512, 512, 4096, 1024, 2048, 1024

def setup_inputs():
    n = np.random.standard_normal
    s = mx_kscale(K)[:, None]
    u = mx_kscale(H)[:, None]
    tab_words, tab_scales = pack_weight(n((K, T)) * s, "e4m3")
    w1 = n((K, H)) / np.sqrt(K) / s * u.T
    w2_words, w2_scales = pack_weight(n((K, H)) / np.sqrt(K) / s * u.T, "e2m1")
    w3 = n((K, H)) / np.sqrt(K) / s * u.T
    w4_words, w4_scales = pack_weight(1.2 * n((H, N)) / np.sqrt(H) / u, "e4m3")
    return {
        "tab_words": tab_words, "tab_scales": tab_scales,
        "offs": striped(np.random.permutation(T)[:S]),
        "offs2": striped(np.random.permutation(T2)[:S]),
        "offs3": striped(np.random.permutation(T2)[:P]),
        "w1": w1.astype(np.float32),
        "w2_words": w2_words, "w2_scales": w2_scales,
        "w3": w3.astype(np.float32),
        "w4_words": w4_words, "w4_scales": w4_scales,
        "page0": (n((H, T2)) * u).astype(np.float32),
        "b": (0.6 * n(N)).astype(np.float32),
    }

def reference(tab_words, tab_scales, offs, offs2, offs3, w1, w2_words, w2_scales, w3, w4_words, w4_scales, page0, b):
    v = unpack_weight(tab_words, tab_scales, "e4m3")[:, unstriped(offs)]
    w2 = unpack_weight(w2_words, w2_scales, "e2m1")
    w4 = unpack_weight(w4_words, w4_scales, "e4m3")
    near = mxq(f64(w1), 0, "e4m3").T @ v
    far = w2.T @ v
    shared = mxq(f64(w3), 0, "e4m3").T @ v
    h = np.maximum(near, far) + shared
    page = f64(page0).copy()
    l2 = unstriped(offs2)
    page[:, l2] = np.maximum(page[:, l2], h)
    x = page[:, unstriped(offs3)]
    y = w4.T @ mxq(x, 0, "e4m3")
    return np.tanh(y + f64(b)[:, None])

@@ -1,0 +1,254 @@
+from contextlib import ExitStack
+
+import concourse.mybir as mybir
+from concourse.masks import make_identity
+
+K, H, N, T, S, T2, M = 1024, 512, 512, 4096, 1024, 2048, 1024
+FLOPS = 2 * (3 * K * H * S + H * N * M)
+
+F32 = mybir.dt.float32
+BF16 = mybir.dt.bfloat16
+I32 = mybir.dt.int32
+U32 = mybir.dt.uint32
+U16 = mybir.dt.uint16
+U8 = mybir.dt.uint8
+FP8X4 = mybir.dt.float8_e4m3fn_x4
+FP4X4 = mybir.dt.float4_e2m1fn_x4
+MAX = mybir.AluOpType.max
+TANH = mybir.ActivationFunctionType.Tanh
+
+P = 128
+PACK = 4
+PASSES = K // (P * PACK)
+QUADS = 4
+JB = S // P
+HALF = S // 2
+PIECE = 256
+PIECES = M // PIECE
+PER_COL = 16
+
+
+def tile_list_siren_audibility_record_kernel(
+    tc, tab_words, tab_scales, offs, offs2, offs3, w1, w2_words, w2_scales, w3, w4_words, w4_scales, page0, b, out
+):
+    nc = tc.nc
+    with ExitStack() as ctx:
+        lists = ctx.enter_context(tc.tile_pool(name="lists", bufs=1))
+        keep = ctx.enter_context(tc.tile_pool(name="keep", bufs=1))
+        big = ctx.enter_context(tc.tile_pool(name="big", bufs=2))
+        ring = ctx.enter_context(tc.tile_pool(name="ring", bufs=2))
+        psum = ctx.enter_context(tc.psum_pool(name="psum", bufs=8))
+
+        idx = lists.tile([P, S // PER_COL], U16, name="idx")
+        idx2 = lists.tile([P, S // PER_COL], U16, name="idx2")
+        idx3 = lists.tile([P, M // PER_COL], U16, name="idx3")
+
+        tab_sc = keep.tile([P, T], U8, name="tab_sc", align_bytes=64)
+        picked_sc = keep.tile([P, S], U8, name="picked_sc", align_bytes=64)
+        v_sc = keep.tile([P, PASSES * S], U8, name="v_sc", align_bytes=64)
+        w2_sc = keep.tile([P, PASSES * H], U8, name="w2_sc", align_bytes=64)
+        w4_sc = keep.tile([P, N], U8, name="w4_sc", align_bytes=64)
+        w2_w = keep.tile([P, PASSES, 2 * H], U8, name="w2_w", align_bytes=64)
+        w4_w = keep.tile([P, N], I32, name="w4_w", align_bytes=64)
+        bias = keep.tile([P, N // P], F32, name="bias")
+        ident = keep.tile([P, P], F32, name="ident")
+        tab_w = [big.tile([P, T], I32, name=f"tab_w{a}", tag="big") for a in range(PASSES)]
+        v_w = [keep.tile([P, S], U32, name=f"v_w{a}", align_bytes=64) for a in range(PASSES)]
+        raw = {(w, a): keep.tile([P, PACK, H], F32, name=f"raw{w}_{a}") for w in (1, 3) for a in range(PASSES)}
+        page = [keep.tile([P, T2], F32, name=f"page{t}") for t in range(PACK)]
+
+        nc.vector.memset(w2_sc[:].bitcast(I32), 0)
+        nc.vector.memset(tab_sc[32:64, :].bitcast(I32), 0)
+        nc.vector.memset(tab_sc[64:128, :].bitcast(I32), 0)
+        nc.vector.memset(v_sc[:].bitcast(I32), 0)
+        nc.vector.memset(w4_sc[:].bitcast(I32), 0)
+
+        def load_weight(w, src, a):
+            rows = src[a * P * PACK : (a + 1) * P * PACK, :]
+            nc.sync.dma_start(raw[w, a][:], rows.rearrange("(p i) c -> p i c", i=PACK))
+
+        def load_page(t):
+            nc.sync.dma_start(page[t][:], page0.rearrange("(p i) c -> p i c", i=PACK)[:, t, :])
+
+        nc.sync.dma_start(idx[:], offs)
+        nc.sync.dma_start(tab_sc[0:32, :].bitcast(I32), tab_scales.rearrange("a q t -> q a t").bitcast(I32))
+        for a in range(PASSES):
+            nc.sync.dma_start(tab_w[a][:], tab_words[a].rearrange("p t i -> p (t i)").bitcast(I32))
+        nc.sync.dma_start(w2_w[:].bitcast(I32), w2_words.rearrange("a p c -> p a c").bitcast(I32))
+        load_weight(1, w1, 0)
+        load_weight(1, w1, 1)
+        load_page(0)
+        nc.sync.dma_start(idx2[:], offs2)
+        load_weight(3, w3, 0)
+        load_weight(3, w3, 1)
+        load_page(1)
+        load_page(2)
+        load_page(3)
+        nc.sync.dma_start(idx3[:], offs3)
+        nc.sync.dma_start(w4_w[:], w4_words[0].rearrange("p c i -> p (c i)").bitcast(I32))
+        for q in range(QUADS):
+            nc.sync.dma_start(
+                w4_sc[32 * q : 32 * q + 4, :].bitcast(I32), w4_scales[0, 4 * q : 4 * q + 4, :].bitcast(I32)
+            )
+        with nc.allow_non_contiguous_dma(reason="one bias value a partition"):
+            nc.sync.dma_start(bias[:], b.rearrange("(c p) -> p c", p=P))
+
+        for q in range(QUADS):
+            nc.gpsimd.dma_start(
+                w2_sc[32 * q : 32 * q + 4, :].rearrange("r (a c) -> r a c", a=PASSES).bitcast(I32),
+                w2_scales[:, 4 * q : 4 * q + 4, :].rearrange("a r c -> r a c").bitcast(I32),
+            )
+
+        nc.vector.tensor_copy(picked_sc[:], tab_sc[:].indirect(idx[:]))
+        for q in range(QUADS):
+            nc.gpsimd.dma_start(v_sc[32 * q : 32 * q + 4, :].bitcast(I32), picked_sc[8 * q : 8 * q + 8, :].bitcast(I32))
+        make_identity(nc, ident[:])
+
+        nc.vector.tensor_copy(v_w[0][:], tab_w[0][:].bitcast(U32).indirect(idx[:]))
+        for u in range(2):
+            cols = slice(u * HALF // PER_COL, (u + 1) * HALF // PER_COL)
+            nc.vector.tensor_copy(v_w[1][:, u * HALF : (u + 1) * HALF], tab_w[1][:].bitcast(U32).indirect(idx[:, cols]))
+
+        def product(jb, moving):
+            acc = psum.tile([P, H], F32, name="acc", tag="bank")
+            for a in range(PASSES):
+                codes, scales = moving(a)
+                nc.tensor.matmul_mx(
+                    acc[:],
+                    lhsT=v_w[a][:, jb * P : (jb + 1) * P].bitcast(FP8X4),
+                    lhsT_scale=v_sc[:, a * S + jb * P : a * S + (jb + 1) * P],
+                    rhs=codes,
+                    rhs_scale=scales,
+                    start=(a == 0),
+                    stop=(a == PASSES - 1),
+                )
+            return acc[:].rearrange("j (m t) -> j t m", t=PACK)
+
+        quantised = {}
+
+        def round_weight(w, a, copy):
+            grouped = keep.tile([P, H, PACK], BF16, name=f"grouped{w}_{a}", align_bytes=64)
+            copy(
+                grouped[:].rearrange("p (c e) i -> p c i e", e=4),
+                raw[w, a][:].rearrange("p i (c e) -> p c i e", e=4),
+            )
+            return grouped
+
+        def quantise_weight(w, a, grouped):
+            codes = keep.tile([P, H], U32, name=f"codes{w}_{a}", align_bytes=64)
+            scales = keep.tile([P, H], U8, name=f"scales{w}_{a}", align_bytes=64)
+            nc.vector.quantize_mx(codes[:].bitcast(FP8X4), scales[:], grouped[:].rearrange("p c i -> p (c i)"))
+            quantised[w, a] = (codes[:].bitcast(FP8X4), scales[:])
+
+        larger = keep.tile([P, JB, PACK, P], F32, name="larger")
+        for jb in range(JB):
+            far = product(jb, lambda a: (w2_w[:, a, :].bitcast(FP4X4), w2_sc[:, a * H : (a + 1) * H]))
+            nc.scalar.copy(larger[:, jb], far)
+
+        for a in range(PASSES):
+            quantise_weight(1, a, round_weight(1, a, nc.vector.tensor_copy))
+        for jb in range(JB):
+            near = product(jb, lambda a: quantised[1, a])
+            nc.vector.tensor_tensor(larger[:, jb], near, larger[:, jb], MAX)
+
+        old = [keep.tile([P, S], F32, name=f"old{t}") for t in range(PACK)]
+
+        def fetch_old(t):
+            nc.vector.tensor_copy(old[t][:], page[t][:].indirect(idx2[:]))
+
+        fetch_old(0)
+        for a in range(PASSES):
+            quantise_weight(3, a, round_weight(3, a, nc.scalar.copy))
+        shared = big.tile([P, JB, PACK, P], F32, name="shared", tag="big")
+        for jb in range(JB):
+            nc.scalar.copy(shared[:, jb], product(jb, lambda a: quantised[3, a]))
+        for t in range(1, PACK):
+            fetch_old(t)
+
+        def features(pair):
+            banks = [psum.tile([P, HALF], F32, name="h", tag="bank") for unit in pair]
+            for i in range(HALF // P):
+                for bank, (t, u) in zip(banks, pair):
+                    jb = u * (HALF // P) + i
+                    for term, src in enumerate((larger, shared)):
+                        nc.tensor.matmul(
+                            bank[:, i * P : (i + 1) * P],
+                            lhsT=src[:, jb, t, :],
+                            rhs=ident[:],
+                            is_transpose=True,
+                            start=(term == 0),
+                            stop=(term == 1),
+                        )
+            return banks
+
+        def raise_old(t, u, bank, new):
+            nc.vector.tensor_tensor(new[:], bank[:], old[t][:, u * HALF : (u + 1) * HALF], MAX)
+
+        def put(t, u, new):
+            cols = slice(u * HALF // PER_COL, (u + 1) * HALF // PER_COL)
+            nc.vector.tensor_copy(page[t][:].indirect(idx2[:, cols]), new[:])
+
+        read = keep.tile([P, PACK - 1, M], BF16, name="read", tag="read")
+
+        def fetch_read(t):
+            nc.vector.tensor_copy(read[:, t, :], page[t][:].indirect(idx3[:]))
+
+        for pair, complete in (
+            (((0, 0), (1, 0)), ()),
+            (((0, 1), (2, 0)), (0,)),
+            (((1, 1), (2, 1)), (1,)),
+        ):
+            banks = features(pair)
+            news = [ring.tile([P, HALF], F32, name="new", tag="new") for unit in pair]
+            for bank, new, (t, u) in zip(banks, news, pair):
+                raise_old(t, u, bank, new)
+            for new, (t, u) in zip(news, pair):
+                put(t, u, new)
+            for t in complete:
+                fetch_read(t)
+
+        last = PACK - 1
+        banks = features(((last, 0), (last, 1)))
+        new = ring.tile([P, HALF], F32, name="new", tag="new")
+        raise_old(last, 0, banks[0], new)
+        fetch_read(last - 1)
+        put(last, 0, new)
+        x = [keep.tile([P, PIECE, PACK], BF16, name=f"x{c}", align_bytes=64) for c in range(PIECES)]
+        for c in range(PIECES):
+            nc.scalar.copy(x[c][:, :, 0:last], read[:, :, c * PIECE : (c + 1) * PIECE].rearrange("p t m -> p m t"))
+        new = keep.tile([P, HALF], F32, name="new_last", tag="read")
+        raise_old(last, 1, banks[1], new)
+        put(last, 1, new)
+
+        result = big.tile([P, N // P, M], F32, name="result", tag="big")
+        out_v = out.rearrange("(n p) m -> p n m", p=P)
+
+        def fetch_last(c):
+            cols = slice(c * PIECE // PER_COL, (c + 1) * PIECE // PER_COL)
+            nc.vector.tensor_copy(x[c][:, :, last], page[last][:].indirect(idx3[:, cols]))
+
+        def finish(c):
+            codes = keep.tile([P, PIECE], U32, name=f"x_codes{c}", align_bytes=64)
+            scales = keep.tile([P, PIECE], U8, name=f"x_scales{c}", align_bytes=64)
+            nc.vector.quantize_mx(codes[:].bitcast(FP8X4), scales[:], x[c][:].rearrange("p m t -> p (m t)"))
+            cols = slice(c * PIECE, (c + 1) * PIECE)
+            for n in range(N // P):
+                y = psum.tile([P, PIECE], F32, name="y", tag="bank")
+                nc.tensor.matmul_mx(
+                    y[:],
+                    lhsT=w4_w[:, n * P : (n + 1) * P].bitcast(FP8X4),
+                    lhsT_scale=w4_sc[:, n * P : (n + 1) * P],
+                    rhs=codes[:].bitcast(FP8X4),
+                    rhs_scale=scales[:],
+                    start=True,
+                    stop=True,
+                )
+                nc.scalar.activation(result[:, n, cols], y[:], TANH, bias=bias[:, n : n + 1])
+                if c == PIECES - 1:
+                    nc.sync.dma_start(out_v[:, n, cols], result[:, n, cols])
+            if c < PIECES - 1:
+                nc.sync.dma_start(out_v[:, :, cols], result[:, :, cols])
+
+        for c in range(PIECES):
+            fetch_last(c)
+            finish(c)

@@ -35,7 +35,7 @@ def tile_list_siren_audibility_record_kernel(
     with ExitStack() as ctx:
         lists = ctx.enter_context(tc.tile_pool(name="lists", bufs=1))
         keep = ctx.enter_context(tc.tile_pool(name="keep", bufs=1))
-        big = ctx.enter_context(tc.tile_pool(name="big", bufs=2))
+        area = ctx.enter_context(tc.tile_pool(name="area", bufs=1))
         ring = ctx.enter_context(tc.tile_pool(name="ring", bufs=2))
         psum = ctx.enter_context(tc.psum_pool(name="psum", bufs=8))
 
@@ -43,71 +43,58 @@ def tile_list_siren_audibility_record_kernel(
         idx2 = lists.tile([P, S // PER_COL], U16, name="idx2")
         idx3 = lists.tile([P, M // PER_COL], U16, name="idx3")
 
-        tab_sc = keep.tile([P, T], U8, name="tab_sc", align_bytes=64)
-        picked_sc = keep.tile([P, S], U8, name="picked_sc", align_bytes=64)
-        v_sc = keep.tile([P, PASSES * S], U8, name="v_sc", align_bytes=64)
-        w2_sc = keep.tile([P, PASSES * H], U8, name="w2_sc", align_bytes=64)
-        w4_sc = keep.tile([P, N], U8, name="w4_sc", align_bytes=64)
-        w2_w = keep.tile([P, PASSES, 2 * H], U8, name="w2_w", align_bytes=64)
-        w4_w = keep.tile([P, N], I32, name="w4_w", align_bytes=64)
-        bias = keep.tile([P, N // P], F32, name="bias")
-        ident = keep.tile([P, P], F32, name="ident")
-        tab_w = [big.tile([P, T], I32, name=f"tab_w{a}", tag="big") for a in range(PASSES)]
-        v_w = [keep.tile([P, S], U32, name=f"v_w{a}", align_bytes=64) for a in range(PASSES)]
-        raw = {(w, a): keep.tile([P, PACK, H], F32, name=f"raw{w}_{a}") for w in (1, 3) for a in range(PASSES)}
-        page = [keep.tile([P, T2], F32, name=f"page{t}") for t in range(PACK)]
+        def tile(shape, dtype, name, tag=None):
+            return keep.tile(shape, dtype, name=name, tag=tag or name, align_bytes=64)
 
-        nc.vector.memset(w2_sc[:].bitcast(I32), 0)
-        nc.vector.memset(tab_sc[32:64, :].bitcast(I32), 0)
-        nc.vector.memset(tab_sc[64:128, :].bitcast(I32), 0)
-        nc.vector.memset(v_sc[:].bitcast(I32), 0)
-        nc.vector.memset(w4_sc[:].bitcast(I32), 0)
+        def placed(shape, dtype, name, kib):
+            return area.tile(shape, dtype, name=name, tag=name, align_bytes=64, offset=kib * 1024)
 
-        def load_weight(w, src, a):
+        tab_sc = tile([P, T], U8, "tab_sc", "A")
+        picked_sc = tile([P, S], U8, "picked_sc", "B")
+        staged_sc = tile([P, S + H], U8, "staged_sc")
+        planes = tile([P, PASSES * (S + H)], U8, "planes")
+        w2_w = tile([P, PASSES, 2 * H], U8, "w2_w", "G")
+        ident = tile([P, P], F32, "ident")
+        tab_w = [tile([P, T], I32, "tab_w0", "E"), placed([P, T], I32, "tab_w1", 4)]
+        v_w = [tile([P, S], U32, f"v_w{a}") for a in range(PASSES)]
+        raw, page = {}, {}
+
+        def load_weight(w, src, a, dest):
             rows = src[a * P * PACK : (a + 1) * P * PACK, :]
-            nc.sync.dma_start(raw[w, a][:], rows.rearrange("(p i) c -> p i c", i=PACK))
+            nc.sync.dma_start(dest[:], rows.rearrange("(p i) c -> p i c", i=PACK))
+            raw[w, a] = dest
 
-        def load_page(t):
-            nc.sync.dma_start(page[t][:], page0.rearrange("(p i) c -> p i c", i=PACK)[:, t, :])
+        def load_page(t, dest):
+            nc.sync.dma_start(dest[:], page0.rearrange("(p i) c -> p i c", i=PACK)[:, t, :])
+            page[t] = dest
 
         nc.sync.dma_start(idx[:], offs)
         nc.sync.dma_start(tab_sc[0:32, :].bitcast(I32), tab_scales.rearrange("a q t -> q a t").bitcast(I32))
+        nc.sync.dma_start(staged_sc[0:32, S:].bitcast(I32), w2_scales.rearrange("a q c -> q a c").bitcast(I32))
+        nc.sync.dma_start(idx2[:], offs2)
+        nc.sync.dma_start(idx3[:], offs3)
         for a in range(PASSES):
             nc.sync.dma_start(tab_w[a][:], tab_words[a].rearrange("p t i -> p (t i)").bitcast(I32))
         nc.sync.dma_start(w2_w[:].bitcast(I32), w2_words.rearrange("a p c -> p a c").bitcast(I32))
-        load_weight(1, w1, 0)
-        load_weight(1, w1, 1)
-        load_page(0)
-        nc.sync.dma_start(idx2[:], offs2)
-        load_weight(3, w3, 0)
-        load_weight(3, w3, 1)
-        load_page(1)
-        load_page(2)
-        load_page(3)
-        nc.sync.dma_start(idx3[:], offs3)
-        nc.sync.dma_start(w4_w[:], w4_words[0].rearrange("p c i -> p (c i)").bitcast(I32))
-        for q in range(QUADS):
-            nc.sync.dma_start(
-                w4_sc[32 * q : 32 * q + 4, :].bitcast(I32), w4_scales[0, 4 * q : 4 * q + 4, :].bitcast(I32)
-            )
-        with nc.allow_non_contiguous_dma(reason="one bias value a partition"):
-            nc.sync.dma_start(bias[:], b.rearrange("(c p) -> p c", p=P))
 
-        for q in range(QUADS):
-            nc.gpsimd.dma_start(
-                w2_sc[32 * q : 32 * q + 4, :].rearrange("r (a c) -> r a c", a=PASSES).bitcast(I32),
-                w2_scales[:, 4 * q : 4 * q + 4, :].rearrange("a r c -> r a c").bitcast(I32),
-            )
-
-        nc.vector.tensor_copy(picked_sc[:], tab_sc[:].indirect(idx[:]))
-        for q in range(QUADS):
-            nc.gpsimd.dma_start(v_sc[32 * q : 32 * q + 4, :].bitcast(I32), picked_sc[8 * q : 8 * q + 8, :].bitcast(I32))
+        nc.vector.memset(tab_sc[32:64, :].bitcast(I32), 0)
+        nc.vector.memset(tab_sc[64:128, :].bitcast(I32), 0)
+        nc.vector.memset(planes[:].bitcast(I32), 0)
         make_identity(nc, ident[:])
 
+        nc.vector.tensor_copy(picked_sc[:], tab_sc[:].indirect(idx[:]))
+        load_weight(1, w1, 0, tile([P, PACK, H], F32, "raw1_0", "A"))
+        nc.vector.tensor_copy(staged_sc[0:32, :S].bitcast(I32), picked_sc[0:32, :].bitcast(I32))
+        for q in range(QUADS):
+            nc.scalar.dma_start(planes[32 * q : 32 * q + 4, :].bitcast(I32), staged_sc[8 * q : 8 * q + 8, :].bitcast(I32))
+        load_weight(1, w1, 1, tile([P, PACK, H], F32, "raw1_1", "B"))
+
         nc.vector.tensor_copy(v_w[0][:], tab_w[0][:].bitcast(U32).indirect(idx[:]))
+        load_page(0, tile([P, T2], F32, "page_0", "E"))
         for u in range(2):
             cols = slice(u * HALF // PER_COL, (u + 1) * HALF // PER_COL)
             nc.vector.tensor_copy(v_w[1][:, u * HALF : (u + 1) * HALF], tab_w[1][:].bitcast(U32).indirect(idx[:, cols]))
+        load_weight(3, w3, 0, placed([P, PACK, H], F32, "raw3_0", 12))
 
         def product(jb, moving):
             acc = psum.tile([P, H], F32, name="acc", tag="bank")
@@ -116,7 +103,7 @@ def tile_list_siren_audibility_record_kernel(
                 nc.tensor.matmul_mx(
                     acc[:],
                     lhsT=v_w[a][:, jb * P : (jb + 1) * P].bitcast(FP8X4),
-                    lhsT_scale=v_sc[:, a * S + jb * P : a * S + (jb + 1) * P],
+                    lhsT_scale=planes[:, a * (S + H) + jb * P : a * (S + H) + (jb + 1) * P],
                     rhs=codes,
                     rhs_scale=scales,
                     start=(a == 0),
@@ -126,44 +113,66 @@ def tile_list_siren_audibility_record_kernel(
 
         quantised = {}
 
-        def round_weight(w, a, copy):
-            grouped = keep.tile([P, H, PACK], BF16, name=f"grouped{w}_{a}", align_bytes=64)
+        def round_weight(w, a, copy, grouped):
             copy(
-                grouped[:].rearrange("p (c e) i -> p c i e", e=4),
+                grouped.rearrange("p (c e) i -> p c i e", e=4),
                 raw[w, a][:].rearrange("p i (c e) -> p c i e", e=4),
             )
-            return grouped
 
-        def quantise_weight(w, a, grouped):
-            codes = keep.tile([P, H], U32, name=f"codes{w}_{a}", align_bytes=64)
-            scales = keep.tile([P, H], U8, name=f"scales{w}_{a}", align_bytes=64)
-            nc.vector.quantize_mx(codes[:].bitcast(FP8X4), scales[:], grouped[:].rearrange("p c i -> p (c i)"))
+        def quantise_weight(w, a, grouped, tag):
+            codes = tile([P, H], U32, f"codes{w}_{a}", tag)
+            scales = tile([P, H], U8, f"scales{w}_{a}")
+            nc.vector.quantize_mx(codes[:].bitcast(FP8X4), scales[:], grouped.rearrange("p c i -> p (c i)"))
             quantised[w, a] = (codes[:].bitcast(FP8X4), scales[:])
 
-        larger = keep.tile([P, JB, PACK, P], F32, name="larger")
+        larger = tile([P, JB, PACK, P], F32, "larger")
         for jb in range(JB):
-            far = product(jb, lambda a: (w2_w[:, a, :].bitcast(FP4X4), w2_sc[:, a * H : (a + 1) * H]))
+            far = product(jb, lambda a: (w2_w[:, a, :].bitcast(FP4X4), planes[:, a * (S + H) + S : (a + 1) * (S + H)]))
             nc.scalar.copy(larger[:, jb], far)
 
-        for a in range(PASSES):
-            quantise_weight(1, a, round_weight(1, a, nc.vector.tensor_copy))
+        grouped1 = [placed([P, H, PACK], BF16, f"grouped1_{a}", 4 + 4 * a) for a in range(PASSES)]
+        round_weight(1, 0, nc.vector.tensor_copy, grouped1[0][:])
+        load_weight(3, w3, 1, tile([P, PACK, H], F32, "raw3_1", "A"))
+        quantise_weight(1, 0, grouped1[0][:], "codes0")
+        load_page(1, placed([P, T2], F32, "page_1", 0))
+        round_weight(1, 1, nc.vector.tensor_copy, grouped1[1][:])
+        load_page(2, tile([P, T2], F32, "page_2", "B"))
+        quantise_weight(1, 1, grouped1[1][:], "codes1")
         for jb in range(JB):
             near = product(jb, lambda a: quantised[1, a])
             nc.vector.tensor_tensor(larger[:, jb], near, larger[:, jb], MAX)
+        load_page(3, tile([P, T2], F32, "page_3", "scales1_1"))
+        w4_w = tile([P, N], I32, "w4_w", "scales1_0")
+        nc.sync.dma_start(w4_w[:], w4_words[0].rearrange("p c i -> p (c i)").bitcast(I32))
 
-        old = [keep.tile([P, S], F32, name=f"old{t}") for t in range(PACK)]
+        old = {}
 
-        def fetch_old(t):
-            nc.vector.tensor_copy(old[t][:], page[t][:].indirect(idx2[:]))
+        def fetch_old(t, dest):
+            nc.vector.tensor_copy(dest, page[t][:].indirect(idx2[:]))
+            old[t] = dest
 
-        fetch_old(0)
+        fetch_old(0, placed([P, S], F32, "old0", 8)[:])
+        grouped3 = tile([P, PASSES, H, PACK], BF16, "grouped3", "G")
         for a in range(PASSES):
-            quantise_weight(3, a, round_weight(3, a, nc.scalar.copy))
-        shared = big.tile([P, JB, PACK, P], F32, name="shared", tag="big")
+            round_weight(3, a, nc.scalar.copy, grouped3[:, a])
+            quantise_weight(3, a, grouped3[:, a], f"codes{1 - a}")
+        shared = tile([P, JB, PACK, P], F32, "shared")
         for jb in range(JB):
             nc.scalar.copy(shared[:, jb], product(jb, lambda a: quantised[3, a]))
-        for t in range(1, PACK):
-            fetch_old(t)
+        old12 = tile([P, 2, S], F32, "old12", "A")
+        fetch_old(1, old12[:, 0, :])
+        fetch_old(2, old12[:, 1, :])
+        fetch_old(3, tile([P, S], F32, "old3", "G")[:])
+
+        w4_sc = tile([P, N], U8, "w4_sc", "scales3_0")
+        nc.gpsimd.memset(w4_sc[:].bitcast(I32), 0)
+        for q in range(QUADS):
+            nc.sync.dma_start(
+                w4_sc[32 * q : 32 * q + 4, :].bitcast(I32), w4_scales[0, 4 * q : 4 * q + 4, :].bitcast(I32)
+            )
+        bias = tile([P, N // P], F32, "bias", "scales3_1")
+        with nc.allow_non_contiguous_dma(reason="one bias value a partition"):
+            nc.sync.dma_start(bias[:], b.rearrange("(c p) -> p c", p=P))
 
         def features(pair):
             banks = [psum.tile([P, HALF], F32, name="h", tag="bank") for unit in pair]
@@ -220,7 +229,7 @@ def tile_list_siren_audibility_record_kernel(
         raise_old(last, 1, banks[1], new)
         put(last, 1, new)
 
-        result = big.tile([P, N // P, M], F32, name="result", tag="big")
+        result = tile([P, N // P, M], F32, "result", "larger")
         out_v = out.rearrange("(n p) m -> p n m", p=P)
 
         def fetch_last(c):

@@ -26,6 +26,7 @@ HALF = S // 2
 PIECE = 256
 PIECES = M // PIECE
 PER_COL = 16
+ROW = S + H + N // 2
 
 
 def tile_list_siren_audibility_record_kernel(
@@ -49,10 +50,10 @@ def tile_list_siren_audibility_record_kernel(
         def placed(shape, dtype, name, kib):
             return area.tile(shape, dtype, name=name, tag=name, align_bytes=64, offset=kib * 1024)
 
-        tab_sc = tile([P, T], U8, "tab_sc", "A")
-        picked_sc = tile([P, S], U8, "picked_sc", "B")
-        staged_sc = tile([P, S + H], U8, "staged_sc")
-        planes = tile([P, PASSES * (S + H)], U8, "planes")
+        tab_sc = tile([P, T], U8, "tab_sc")
+        picked_sc = placed([P, S], U8, "picked_sc", 4)
+        staged_sc = tile([P, ROW], U8, "staged_sc", "B")
+        planes = tile([P, PASSES * ROW], U8, "planes")
         w2_w = tile([P, PASSES, 2 * H], U8, "w2_w", "G")
         ident = tile([P, P], F32, "ident")
         tab_w = [tile([P, T], I32, "tab_w0", "E"), placed([P, T], I32, "tab_w1", 4)]
@@ -70,12 +71,15 @@ def tile_list_siren_audibility_record_kernel(
 
         nc.sync.dma_start(idx[:], offs)
         nc.sync.dma_start(tab_sc[0:32, :].bitcast(I32), tab_scales.rearrange("a q t -> q a t").bitcast(I32))
-        nc.sync.dma_start(staged_sc[0:32, S:].bitcast(I32), w2_scales.rearrange("a q c -> q a c").bitcast(I32))
+        nc.sync.dma_start(staged_sc[0:32, S : S + H].bitcast(I32), w2_scales.rearrange("a q c -> q a c").bitcast(I32))
+        nc.sync.dma_start(
+            staged_sc[0:32, S + H :].bitcast(I32), w4_scales[0].rearrange("q (a c) -> (q a) c", a=2).bitcast(I32)
+        )
         nc.sync.dma_start(idx2[:], offs2)
         nc.sync.dma_start(idx3[:], offs3)
-        for a in range(PASSES):
-            nc.sync.dma_start(tab_w[a][:], tab_words[a].rearrange("p t i -> p (t i)").bitcast(I32))
+        nc.sync.dma_start(tab_w[0][:], tab_words[0].rearrange("p t i -> p (t i)").bitcast(I32))
         nc.sync.dma_start(w2_w[:].bitcast(I32), w2_words.rearrange("a p c -> p a c").bitcast(I32))
+        load_weight(1, w1, 0, tile([P, PACK, H], F32, "raw1_0", "A"))
 
         nc.vector.memset(tab_sc[32:64, :].bitcast(I32), 0)
         nc.vector.memset(tab_sc[64:128, :].bitcast(I32), 0)
@@ -83,34 +87,13 @@ def tile_list_siren_audibility_record_kernel(
         make_identity(nc, ident[:])
 
         nc.vector.tensor_copy(picked_sc[:], tab_sc[:].indirect(idx[:]))
-        load_weight(1, w1, 0, tile([P, PACK, H], F32, "raw1_0", "A"))
         nc.vector.tensor_copy(staged_sc[0:32, :S].bitcast(I32), picked_sc[0:32, :].bitcast(I32))
         for q in range(QUADS):
-            nc.scalar.dma_start(planes[32 * q : 32 * q + 4, :].bitcast(I32), staged_sc[8 * q : 8 * q + 8, :].bitcast(I32))
+            nc.sync.dma_start(planes[32 * q : 32 * q + 4, :].bitcast(I32), staged_sc[8 * q : 8 * q + 8, :].bitcast(I32))
+        nc.sync.dma_start(tab_w[1][:], tab_words[1].rearrange("p t i -> p (t i)").bitcast(I32))
         load_weight(1, w1, 1, tile([P, PACK, H], F32, "raw1_1", "B"))
 
         nc.vector.tensor_copy(v_w[0][:], tab_w[0][:].bitcast(U32).indirect(idx[:]))
-        load_page(0, tile([P, T2], F32, "page_0", "E"))
-        for u in range(2):
-            cols = slice(u * HALF // PER_COL, (u + 1) * HALF // PER_COL)
-            nc.vector.tensor_copy(v_w[1][:, u * HALF : (u + 1) * HALF], tab_w[1][:].bitcast(U32).indirect(idx[:, cols]))
-        load_weight(3, w3, 0, placed([P, PACK, H], F32, "raw3_0", 12))
-
-        def product(jb, moving):
-            acc = psum.tile([P, H], F32, name="acc", tag="bank")
-            for a in range(PASSES):
-                codes, scales = moving(a)
-                nc.tensor.matmul_mx(
-                    acc[:],
-                    lhsT=v_w[a][:, jb * P : (jb + 1) * P].bitcast(FP8X4),
-                    lhsT_scale=planes[:, a * (S + H) + jb * P : a * (S + H) + (jb + 1) * P],
-                    rhs=codes,
-                    rhs_scale=scales,
-                    start=(a == 0),
-                    stop=(a == PASSES - 1),
-                )
-            return acc[:].rearrange("j (m t) -> j t m", t=PACK)
-
         quantised = {}
 
         def round_weight(w, a, copy, grouped):
@@ -125,19 +108,41 @@ def tile_list_siren_audibility_record_kernel(
             nc.vector.quantize_mx(codes[:].bitcast(FP8X4), scales[:], grouped.rearrange("p c i -> p (c i)"))
             quantised[w, a] = (codes[:].bitcast(FP8X4), scales[:])
 
+        grouped = tile([P, H, PACK], BF16, "grouped1_0", "E")
+        round_weight(1, 0, nc.vector.tensor_copy, grouped[:])
+        load_weight(3, w3, 0, tile([P, PACK, H], F32, "raw3_0", "A"))
+        quantise_weight(1, 0, grouped[:], "codes0")
+        load_weight(3, w3, 1, tile([P, PACK, H], F32, "raw3_1", "E"))
+        for u in range(2):
+            cols = slice(u * HALF // PER_COL, (u + 1) * HALF // PER_COL)
+            nc.vector.tensor_copy(v_w[1][:, u * HALF : (u + 1) * HALF], tab_w[1][:].bitcast(U32).indirect(idx[:, cols]))
+        load_page(0, placed([P, T2], F32, "page_0", 0))
+        load_page(1, placed([P, T2], F32, "page_1", 12))
+
+        def product(jb, moving):
+            acc = psum.tile([P, H], F32, name="acc", tag="bank")
+            for a in range(PASSES):
+                codes, scales = moving(a)
+                nc.tensor.matmul_mx(
+                    acc[:],
+                    lhsT=v_w[a][:, jb * P : (jb + 1) * P].bitcast(FP8X4),
+                    lhsT_scale=planes[:, a * ROW + jb * P : a * ROW + (jb + 1) * P],
+                    rhs=codes,
+                    rhs_scale=scales,
+                    start=(a == 0),
+                    stop=(a == PASSES - 1),
+                )
+            return acc[:].rearrange("j (m t) -> j t m", t=PACK)
+
         larger = tile([P, JB, PACK, P], F32, "larger")
         for jb in range(JB):
-            far = product(jb, lambda a: (w2_w[:, a, :].bitcast(FP4X4), planes[:, a * (S + H) + S : (a + 1) * (S + H)]))
+            far = product(jb, lambda a: (w2_w[:, a, :].bitcast(FP4X4), planes[:, a * ROW + S : a * ROW + S + H]))
             nc.scalar.copy(larger[:, jb], far)
 
-        grouped1 = [placed([P, H, PACK], BF16, f"grouped1_{a}", 4 + 4 * a) for a in range(PASSES)]
-        round_weight(1, 0, nc.vector.tensor_copy, grouped1[0][:])
-        load_weight(3, w3, 1, tile([P, PACK, H], F32, "raw3_1", "A"))
-        quantise_weight(1, 0, grouped1[0][:], "codes0")
-        load_page(1, placed([P, T2], F32, "page_1", 0))
-        round_weight(1, 1, nc.vector.tensor_copy, grouped1[1][:])
+        grouped = placed([P, H, PACK], BF16, "grouped1_1", 8)
+        round_weight(1, 1, nc.vector.tensor_copy, grouped[:])
         load_page(2, tile([P, T2], F32, "page_2", "B"))
-        quantise_weight(1, 1, grouped1[1][:], "codes1")
+        quantise_weight(1, 1, grouped[:], "codes1")
         for jb in range(JB):
             near = product(jb, lambda a: quantised[1, a])
             nc.vector.tensor_tensor(larger[:, jb], near, larger[:, jb], MAX)
@@ -151,7 +156,6 @@ def tile_list_siren_audibility_record_kernel(
             nc.vector.tensor_copy(dest, page[t][:].indirect(idx2[:]))
             old[t] = dest
 
-        fetch_old(0, placed([P, S], F32, "old0", 8)[:])
         grouped3 = tile([P, PASSES, H, PACK], BF16, "grouped3", "G")
         for a in range(PASSES):
             round_weight(3, a, nc.scalar.copy, grouped3[:, a])
@@ -159,17 +163,12 @@ def tile_list_siren_audibility_record_kernel(
         shared = tile([P, JB, PACK, P], F32, "shared")
         for jb in range(JB):
             nc.scalar.copy(shared[:, jb], product(jb, lambda a: quantised[3, a]))
-        old12 = tile([P, 2, S], F32, "old12", "A")
-        fetch_old(1, old12[:, 0, :])
-        fetch_old(2, old12[:, 1, :])
+        old01 = tile([P, 2, S], F32, "old01", "E")
+        fetch_old(0, old01[:, 0, :])
+        fetch_old(1, old01[:, 1, :])
+        fetch_old(2, tile([P, S], F32, "old2", "A")[:])
         fetch_old(3, tile([P, S], F32, "old3", "G")[:])
 
-        w4_sc = tile([P, N], U8, "w4_sc", "scales3_0")
-        nc.gpsimd.memset(w4_sc[:].bitcast(I32), 0)
-        for q in range(QUADS):
-            nc.sync.dma_start(
-                w4_sc[32 * q : 32 * q + 4, :].bitcast(I32), w4_scales[0, 4 * q : 4 * q + 4, :].bitcast(I32)
-            )
         bias = tile([P, N // P], F32, "bias", "scales3_1")
         with nc.allow_non_contiguous_dma(reason="one bias value a partition"):
             nc.sync.dma_start(bias[:], b.rearrange("(c p) -> p c", p=P))
@@ -220,7 +219,9 @@ def tile_list_siren_audibility_record_kernel(
         banks = features(((last, 0), (last, 1)))
         new = ring.tile([P, HALF], F32, name="new", tag="new")
         raise_old(last, 0, banks[0], new)
-        fetch_read(last - 1)
+        for u in range(2):
+            cols = slice(u * HALF // PER_COL, (u + 1) * HALF // PER_COL)
+            nc.vector.tensor_copy(read[:, last - 1, u * HALF : (u + 1) * HALF], page[last - 1][:].indirect(idx3[:, cols]))
         put(last, 0, new)
         x = [keep.tile([P, PIECE, PACK], BF16, name=f"x{c}", align_bytes=64) for c in range(PIECES)]
         for c in range(PIECES):
@@ -242,11 +243,12 @@ def tile_list_siren_audibility_record_kernel(
             nc.vector.quantize_mx(codes[:].bitcast(FP8X4), scales[:], x[c][:].rearrange("p m t -> p (m t)"))
             cols = slice(c * PIECE, (c + 1) * PIECE)
             for n in range(N // P):
+                w4_col = n // 2 * ROW + S + H + n % 2 * P
                 y = psum.tile([P, PIECE], F32, name="y", tag="bank")
                 nc.tensor.matmul_mx(
                     y[:],
                     lhsT=w4_w[:, n * P : (n + 1) * P].bitcast(FP8X4),
-                    lhsT_scale=w4_sc[:, n * P : (n + 1) * P],
+                    lhsT_scale=planes[:, w4_col : w4_col + P],
                     rhs=codes[:].bitcast(FP8X4),
                     rhs_scale=scales[:],
                     start=True,

@@ -21,12 +21,19 @@ P = 128
 PACK = 4
 PASSES = K // (P * PACK)
 QUADS = 4
-JB = S // P
+BLOCKS = S // P
 HALF = S // 2
 PIECE = 256
 PIECES = M // PIECE
 PER_COL = 16
 ROW = S + H + N // 2
+SPLIT = 352
+RUN = 4
+LAST = PACK - 1
+
+
+def entries(start, count):
+    return slice(start // PER_COL, (start + count) // PER_COL)
 
 
 def tile_list_siren_audibility_record_kernel(
@@ -44,19 +51,19 @@ def tile_list_siren_audibility_record_kernel(
         idx2 = lists.tile([P, S // PER_COL], U16, name="idx2")
         idx3 = lists.tile([P, M // PER_COL], U16, name="idx3")
 
-        def tile(shape, dtype, name, tag=None):
-            return keep.tile(shape, dtype, name=name, tag=tag or name, align_bytes=64)
+        def tile(shape, dtype, name, over=None):
+            return keep.tile(shape, dtype, name=name, tag=over or name, align_bytes=64)
 
         def placed(shape, dtype, name, kib):
             return area.tile(shape, dtype, name=name, tag=name, align_bytes=64, offset=kib * 1024)
 
         tab_sc = tile([P, T], U8, "tab_sc")
         picked_sc = placed([P, S], U8, "picked_sc", 4)
-        staged_sc = tile([P, ROW], U8, "staged_sc", "B")
+        staged_sc = tile([P, ROW], U8, "staged_sc")
         planes = tile([P, PASSES * ROW], U8, "planes")
-        w2_w = tile([P, PASSES, 2 * H], U8, "w2_w", "G")
+        w2_w = tile([P, PASSES, 2 * H], U8, "w2_w")
         ident = tile([P, P], F32, "ident")
-        tab_w = [tile([P, T], I32, "tab_w0", "E"), placed([P, T], I32, "tab_w1", 4)]
+        tab_w = [tile([P, T], I32, "tab_w0"), placed([P, T], I32, "tab_w1", 4)]
         v_w = [tile([P, S], U32, f"v_w{a}") for a in range(PASSES)]
         raw, page = {}, {}
 
@@ -79,7 +86,7 @@ def tile_list_siren_audibility_record_kernel(
         nc.sync.dma_start(idx3[:], offs3)
         nc.sync.dma_start(tab_w[0][:], tab_words[0].rearrange("p t i -> p (t i)").bitcast(I32))
         nc.sync.dma_start(w2_w[:].bitcast(I32), w2_words.rearrange("a p c -> p a c").bitcast(I32))
-        load_weight(1, w1, 0, tile([P, PACK, H], F32, "raw1_0", "A"))
+        load_weight(1, w1, 0, tile([P, PACK, H], F32, "raw1_0"))
 
         nc.vector.memset(tab_sc[32:64, :].bitcast(I32), 0)
         nc.vector.memset(tab_sc[64:128, :].bitcast(I32), 0)
@@ -88,36 +95,36 @@ def tile_list_siren_audibility_record_kernel(
 
         nc.vector.tensor_copy(picked_sc[:], tab_sc[:].indirect(idx[:]))
         nc.vector.tensor_copy(staged_sc[0:32, :S].bitcast(I32), picked_sc[0:32, :].bitcast(I32))
-        for q in range(QUADS):
-            nc.sync.dma_start(planes[32 * q : 32 * q + 4, :].bitcast(I32), staged_sc[8 * q : 8 * q + 8, :].bitcast(I32))
+        for g in range(QUADS):
+            nc.sync.dma_start(planes[32 * g : 32 * g + 4, :].bitcast(I32), staged_sc[8 * g : 8 * g + 8, :].bitcast(I32))
         nc.sync.dma_start(tab_w[1][:], tab_words[1].rearrange("p t i -> p (t i)").bitcast(I32))
-        load_weight(1, w1, 1, tile([P, PACK, H], F32, "raw1_1", "B"))
+        load_weight(1, w1, 1, tile([P, PACK, H], F32, "raw1_1", over="staged_sc"))
 
         nc.vector.tensor_copy(v_w[0][:], tab_w[0][:].bitcast(U32).indirect(idx[:]))
         quantised = {}
 
-        def round_weight(w, a, copy, grouped):
+        def round_weight(w, a, copy, grouped, cols=slice(0, H)):
             copy(
-                grouped.rearrange("p (c e) i -> p c i e", e=4),
-                raw[w, a][:].rearrange("p i (c e) -> p c i e", e=4),
+                grouped[:, cols, :].rearrange("p (c e) i -> p c i e", e=RUN),
+                raw[w, a][:, :, cols].rearrange("p i (c e) -> p c i e", e=RUN),
             )
 
-        def quantise_weight(w, a, grouped, tag):
-            codes = tile([P, H], U32, f"codes{w}_{a}", tag)
+        def quantise_weight(w, a, grouped, over=None):
+            codes = tile([P, H], U32, f"codes{w}_{a}", over)
             scales = tile([P, H], U8, f"scales{w}_{a}")
             nc.vector.quantize_mx(codes[:].bitcast(FP8X4), scales[:], grouped.rearrange("p c i -> p (c i)"))
             quantised[w, a] = (codes[:].bitcast(FP8X4), scales[:])
 
-        grouped = tile([P, H, PACK], BF16, "grouped1_0", "E")
-        round_weight(1, 0, nc.vector.tensor_copy, grouped[:])
-        load_weight(3, w3, 0, tile([P, PACK, H], F32, "raw3_0", "A"))
-        quantise_weight(1, 0, grouped[:], "codes0")
-        load_weight(3, w3, 1, tile([P, PACK, H], F32, "raw3_1", "E"))
+        grouped1_0 = tile([P, H, PACK], BF16, "grouped1_0", over="tab_w0")
+        round_weight(1, 0, nc.vector.tensor_copy, grouped1_0[:])
+        load_weight(3, w3, 0, tile([P, PACK, H], F32, "raw3_0", over="raw1_0"))
+        quantise_weight(1, 0, grouped1_0[:])
+        load_weight(3, w3, 1, tile([P, PACK, H], F32, "raw3_1", over="tab_w0"))
         for u in range(2):
-            cols = slice(u * HALF // PER_COL, (u + 1) * HALF // PER_COL)
-            nc.vector.tensor_copy(v_w[1][:, u * HALF : (u + 1) * HALF], tab_w[1][:].bitcast(U32).indirect(idx[:, cols]))
-        load_page(0, placed([P, T2], F32, "page_0", 0))
-        load_page(1, placed([P, T2], F32, "page_1", 12))
+            window = tab_w[1][:].bitcast(U32)
+            nc.vector.tensor_copy(v_w[1][:, u * HALF : (u + 1) * HALF], window.indirect(idx[:, entries(u * HALF, HALF)]))
+        load_page(2, placed([P, T2], F32, "page_2", 0))
+        load_page(0, placed([P, T2], F32, "page_0", 12))
 
         def product(jb, moving):
             acc = psum.tile([P, H], F32, name="acc", tag="bank")
@@ -134,20 +141,22 @@ def tile_list_siren_audibility_record_kernel(
                 )
             return acc[:].rearrange("j (m t) -> j t m", t=PACK)
 
-        larger = tile([P, JB, PACK, P], F32, "larger")
-        for jb in range(JB):
+        grouped1_1 = placed([P, H, PACK], BF16, "grouped1_1", 8)
+        round_weight(1, 1, nc.vector.tensor_copy, grouped1_1[:], slice(0, SPLIT))
+        round_weight(1, 1, nc.scalar.copy, grouped1_1[:], slice(SPLIT, H))
+
+        larger = tile([P, BLOCKS, PACK, P], F32, "larger")
+        for jb in range(BLOCKS):
             far = product(jb, lambda a: (w2_w[:, a, :].bitcast(FP4X4), planes[:, a * ROW + S : a * ROW + S + H]))
             nc.scalar.copy(larger[:, jb], far)
 
-        grouped = placed([P, H, PACK], BF16, "grouped1_1", 8)
-        round_weight(1, 1, nc.vector.tensor_copy, grouped[:])
-        load_page(2, tile([P, T2], F32, "page_2", "B"))
-        quantise_weight(1, 1, grouped[:], "codes1")
-        for jb in range(JB):
+        load_page(1, tile([P, T2], F32, "page_1", over="staged_sc"))
+        quantise_weight(1, 1, grouped1_1[:])
+        for jb in range(BLOCKS):
             near = product(jb, lambda a: quantised[1, a])
             nc.vector.tensor_tensor(larger[:, jb], near, larger[:, jb], MAX)
-        load_page(3, tile([P, T2], F32, "page_3", "scales1_1"))
-        w4_w = tile([P, N], I32, "w4_w", "scales1_0")
+        load_page(LAST, tile([P, T2], F32, "page_3", over="scales1_1"))
+        w4_w = tile([P, N], I32, "w4_w", over="scales1_0")
         nc.sync.dma_start(w4_w[:], w4_words[0].rearrange("p c i -> p (c i)").bitcast(I32))
 
         old = {}
@@ -156,25 +165,26 @@ def tile_list_siren_audibility_record_kernel(
             nc.vector.tensor_copy(dest, page[t][:].indirect(idx2[:]))
             old[t] = dest
 
-        grouped3 = tile([P, PASSES, H, PACK], BF16, "grouped3", "G")
-        for a in range(PASSES):
-            round_weight(3, a, nc.scalar.copy, grouped3[:, a])
-            quantise_weight(3, a, grouped3[:, a], f"codes{1 - a}")
-        shared = tile([P, JB, PACK, P], F32, "shared")
-        for jb in range(JB):
+        grouped3 = tile([P, PASSES, H, PACK], BF16, "grouped3", over="w2_w")
+        round_weight(3, 0, nc.scalar.copy, grouped3[:, 0])
+        quantise_weight(3, 0, grouped3[:, 0], over="codes1_1")
+        fetch_old(2, tile([P, S], F32, "old2", over="raw1_0")[:])
+        round_weight(3, 1, nc.scalar.copy, grouped3[:, 1])
+        quantise_weight(3, 1, grouped3[:, 1], over="codes1_0")
+        shared = tile([P, BLOCKS, PACK, P], F32, "shared")
+        for jb in range(BLOCKS):
             nc.scalar.copy(shared[:, jb], product(jb, lambda a: quantised[3, a]))
-        old01 = tile([P, 2, S], F32, "old01", "E")
+        old01 = tile([P, 2, S], F32, "old01", over="tab_w0")
         fetch_old(0, old01[:, 0, :])
         fetch_old(1, old01[:, 1, :])
-        fetch_old(2, tile([P, S], F32, "old2", "A")[:])
-        fetch_old(3, tile([P, S], F32, "old3", "G")[:])
+        fetch_old(LAST, tile([P, S], F32, "old3", over="w2_w")[:])
 
-        bias = tile([P, N // P], F32, "bias", "scales3_1")
+        bias = tile([P, N // P], F32, "bias", over="scales3_1")
         with nc.allow_non_contiguous_dma(reason="one bias value a partition"):
             nc.sync.dma_start(bias[:], b.rearrange("(c p) -> p c", p=P))
 
         def features(pair):
-            banks = [psum.tile([P, HALF], F32, name="h", tag="bank") for unit in pair]
+            banks = [psum.tile([P, HALF], F32, name="h", tag="bank") for half in pair]
             for i in range(HALF // P):
                 for bank, (t, u) in zip(banks, pair):
                     jb = u * (HALF // P) + i
@@ -189,53 +199,48 @@ def tile_list_siren_audibility_record_kernel(
                         )
             return banks
 
-        def raise_old(t, u, bank, new):
-            nc.vector.tensor_tensor(new[:], bank[:], old[t][:, u * HALF : (u + 1) * HALF], MAX)
-
         def put(t, u, new):
-            cols = slice(u * HALF // PER_COL, (u + 1) * HALF // PER_COL)
-            nc.vector.tensor_copy(page[t][:].indirect(idx2[:, cols]), new[:])
+            nc.vector.tensor_copy(page[t][:].indirect(idx2[:, entries(u * HALF, HALF)]), new[:])
 
-        read = keep.tile([P, PACK - 1, M], BF16, name="read", tag="read")
-
-        def fetch_read(t):
-            nc.vector.tensor_copy(read[:, t, :], page[t][:].indirect(idx3[:]))
-
-        for pair, complete in (
-            (((0, 0), (1, 0)), ()),
-            (((0, 1), (2, 0)), (0,)),
-            (((1, 1), (2, 1)), (1,)),
-        ):
+        def update(pair, between=None):
             banks = features(pair)
-            news = [ring.tile([P, HALF], F32, name="new", tag="new") for unit in pair]
+            news = [ring.tile([P, HALF], F32, name="new", tag="new") for half in pair]
             for bank, new, (t, u) in zip(banks, news, pair):
-                raise_old(t, u, bank, new)
-            for new, (t, u) in zip(news, pair):
-                put(t, u, new)
-            for t in complete:
-                fetch_read(t)
+                nc.vector.tensor_tensor(new[:], bank[:], old[t][:, u * HALF : (u + 1) * HALF], MAX)
+            put(*pair[0], news[0])
+            if between is not None:
+                between()
+            put(*pair[1], news[1])
 
-        last = PACK - 1
-        banks = features(((last, 0), (last, 1)))
-        new = ring.tile([P, HALF], F32, name="new", tag="new")
-        raise_old(last, 0, banks[0], new)
-        for u in range(2):
-            cols = slice(u * HALF // PER_COL, (u + 1) * HALF // PER_COL)
-            nc.vector.tensor_copy(read[:, last - 1, u * HALF : (u + 1) * HALF], page[last - 1][:].indirect(idx3[:, cols]))
-        put(last, 0, new)
-        x = [keep.tile([P, PIECE, PACK], BF16, name=f"x{c}", align_bytes=64) for c in range(PIECES)]
+        def fetch_read(t, dest):
+            nc.vector.tensor_copy(dest, page[t][:].indirect(idx3[:]))
+
+        x = [tile([P, PIECE, PACK], BF16, f"x{c}") for c in range(PIECES)]
+
+        update(((2, 0), (0, 0)))
+        update(((2, 1), (1, 0)))
+        read2 = tile([P, M], BF16, "read2")
+        fetch_read(2, read2[:])
         for c in range(PIECES):
-            nc.scalar.copy(x[c][:, :, 0:last], read[:, :, c * PIECE : (c + 1) * PIECE].rearrange("p t m -> p m t"))
-        new = keep.tile([P, HALF], F32, name="new_last", tag="read")
-        raise_old(last, 1, banks[1], new)
-        put(last, 1, new)
+            nc.scalar.copy(x[c][:, :, 2], read2[:, c * PIECE : (c + 1) * PIECE])
+        update(((0, 1), (1, 1)))
+        read01 = tile([P, 2, M], BF16, "read01", over="read2")
+        fetch_read(0, read01[:, 0, :])
+        update(((LAST, 0), (LAST, 1)), lambda: fetch_read(1, read01[:, 1, :]))
+        for c in range(PIECES):
+            nc.scalar.copy(x[c][:, :, 0:2], read01[:, :, c * PIECE : (c + 1) * PIECE].rearrange("p t m -> p m t"))
 
-        result = tile([P, N // P, M], F32, "result", "larger")
+        result = tile([P, N // P, M], F32, "result", over="larger")
         out_v = out.rearrange("(n p) m -> p n m", p=P)
 
         def fetch_last(c):
-            cols = slice(c * PIECE // PER_COL, (c + 1) * PIECE // PER_COL)
-            nc.vector.tensor_copy(x[c][:, :, last], page[last][:].indirect(idx3[:, cols]))
+            picked = page[LAST][:].indirect(idx3[:, entries(c * PIECE, PIECE)])
+            if c < 2:
+                nc.vector.tensor_copy(x[c][:, :, LAST], picked)
+            else:
+                value3 = tile([P, PIECE], BF16, f"value3_{c}", over=f"x{c - 2}")
+                nc.vector.tensor_copy(value3[:], picked)
+                nc.vector.tensor_copy(x[c][:, :, LAST], value3[:])
 
         def finish(c):
             codes = keep.tile([P, PIECE], U32, name=f"x_codes{c}", align_bytes=64)
@@ -255,10 +260,7 @@ def tile_list_siren_audibility_record_kernel(
                     stop=True,
                 )
                 nc.scalar.activation(result[:, n, cols], y[:], TANH, bias=bias[:, n : n + 1])
-                if c == PIECES - 1:
-                    nc.sync.dma_start(out_v[:, n, cols], result[:, n, cols])
-            if c < PIECES - 1:
-                nc.sync.dma_start(out_v[:, :, cols], result[:, :, cols])
+                nc.sync.dma_start(out_v[:, n, cols], result[:, n, cols])
 
         for c in range(PIECES):
             fetch_last(c)

from contextlib import ExitStack

import concourse.mybir as mybir
from concourse.masks import make_identity

K, H, N, T, S, T2, M = 1024, 512, 512, 4096, 1024, 2048, 1024
FLOPS = 2 * (3 * K * H * S + H * N * M)

F32 = mybir.dt.float32
BF16 = mybir.dt.bfloat16
I32 = mybir.dt.int32
U32 = mybir.dt.uint32
U16 = mybir.dt.uint16
U8 = mybir.dt.uint8
FP8X4 = mybir.dt.float8_e4m3fn_x4
FP4X4 = mybir.dt.float4_e2m1fn_x4
MAX = mybir.AluOpType.max
TANH = mybir.ActivationFunctionType.Tanh

P = 128
PACK = 4
PASSES = K // (P * PACK)
QUADS = 4
BLOCKS = S // P
HALF = S // 2
PIECE = 256
PIECES = M // PIECE
PER_COL = 16
ROW = S + H + N // 2
SPLIT = 352
RUN = 4
LAST = PACK - 1


def entries(start, count):
    return slice(start // PER_COL, (start + count) // PER_COL)


def tile_list_siren_audibility_record_kernel(
    tc, tab_words, tab_scales, offs, offs2, offs3, w1, w2_words, w2_scales, w3, w4_words, w4_scales, page0, b, out
):
    nc = tc.nc
    with ExitStack() as ctx:
        lists = ctx.enter_context(tc.tile_pool(name="lists", bufs=1))
        keep = ctx.enter_context(tc.tile_pool(name="keep", bufs=1))
        area = ctx.enter_context(tc.tile_pool(name="area", bufs=1))
        ring = ctx.enter_context(tc.tile_pool(name="ring", bufs=2))
        psum = ctx.enter_context(tc.psum_pool(name="psum", bufs=8))

        idx = lists.tile([P, S // PER_COL], U16, name="idx")
        idx2 = lists.tile([P, S // PER_COL], U16, name="idx2")
        idx3 = lists.tile([P, M // PER_COL], U16, name="idx3")

        def tile(shape, dtype, name, over=None):
            return keep.tile(shape, dtype, name=name, tag=over or name, align_bytes=64)

        def placed(shape, dtype, name, kib):
            return area.tile(shape, dtype, name=name, tag=name, align_bytes=64, offset=kib * 1024)

        tab_sc = tile([P, T], U8, "tab_sc")
        picked_sc = placed([P, S], U8, "picked_sc", 4)
        staged_sc = tile([P, ROW], U8, "staged_sc")
        planes = tile([P, PASSES * ROW], U8, "planes")
        w2_w = tile([P, PASSES, 2 * H], U8, "w2_w")
        ident = tile([P, P], F32, "ident")
        tab_w = [tile([P, T], I32, "tab_w0"), placed([P, T], I32, "tab_w1", 4)]
        v_w = [tile([P, S], U32, f"v_w{a}") for a in range(PASSES)]
        raw, page = {}, {}

        def load_weight(w, src, a, dest):
            rows = src[a * P * PACK : (a + 1) * P * PACK, :]
            nc.sync.dma_start(dest[:], rows.rearrange("(p i) c -> p i c", i=PACK))
            raw[w, a] = dest

        def load_page(t, dest):
            nc.sync.dma_start(dest[:], page0.rearrange("(p i) c -> p i c", i=PACK)[:, t, :])
            page[t] = dest

        nc.sync.dma_start(idx[:], offs)
        nc.sync.dma_start(tab_sc[0:32, :].bitcast(I32), tab_scales.rearrange("a q t -> q a t").bitcast(I32))
        nc.sync.dma_start(staged_sc[0:32, S : S + H].bitcast(I32), w2_scales.rearrange("a q c -> q a c").bitcast(I32))
        nc.sync.dma_start(
            staged_sc[0:32, S + H :].bitcast(I32), w4_scales[0].rearrange("q (a c) -> (q a) c", a=2).bitcast(I32)
        )
        nc.sync.dma_start(idx2[:], offs2)
        nc.sync.dma_start(idx3[:], offs3)
        nc.sync.dma_start(tab_w[0][:], tab_words[0].rearrange("p t i -> p (t i)").bitcast(I32))
        nc.sync.dma_start(w2_w[:].bitcast(I32), w2_words.rearrange("a p c -> p a c").bitcast(I32))
        load_weight(1, w1, 0, tile([P, PACK, H], F32, "raw1_0"))

        nc.vector.memset(tab_sc[32:64, :].bitcast(I32), 0)
        nc.vector.memset(tab_sc[64:128, :].bitcast(I32), 0)
        nc.vector.memset(planes[:].bitcast(I32), 0)
        make_identity(nc, ident[:])

        nc.vector.tensor_copy(picked_sc[:], tab_sc[:].indirect(idx[:]))
        nc.vector.tensor_copy(staged_sc[0:32, :S].bitcast(I32), picked_sc[0:32, :].bitcast(I32))
        for g in range(QUADS):
            nc.sync.dma_start(planes[32 * g : 32 * g + 4, :].bitcast(I32), staged_sc[8 * g : 8 * g + 8, :].bitcast(I32))
        nc.sync.dma_start(tab_w[1][:], tab_words[1].rearrange("p t i -> p (t i)").bitcast(I32))
        load_weight(1, w1, 1, tile([P, PACK, H], F32, "raw1_1", over="staged_sc"))

        nc.vector.tensor_copy(v_w[0][:], tab_w[0][:].bitcast(U32).indirect(idx[:]))
        quantised = {}

        def round_weight(w, a, copy, grouped, cols=slice(0, H)):
            copy(
                grouped[:, cols, :].rearrange("p (c e) i -> p c i e", e=RUN),
                raw[w, a][:, :, cols].rearrange("p i (c e) -> p c i e", e=RUN),
            )

        def quantise_weight(w, a, grouped, over=None):
            codes = tile([P, H], U32, f"codes{w}_{a}", over)
            scales = tile([P, H], U8, f"scales{w}_{a}")
            nc.vector.quantize_mx(codes[:].bitcast(FP8X4), scales[:], grouped.rearrange("p c i -> p (c i)"))
            quantised[w, a] = (codes[:].bitcast(FP8X4), scales[:])

        grouped1_0 = tile([P, H, PACK], BF16, "grouped1_0", over="tab_w0")
        round_weight(1, 0, nc.vector.tensor_copy, grouped1_0[:])
        load_weight(3, w3, 0, tile([P, PACK, H], F32, "raw3_0", over="raw1_0"))
        quantise_weight(1, 0, grouped1_0[:])
        load_weight(3, w3, 1, tile([P, PACK, H], F32, "raw3_1", over="tab_w0"))
        for u in range(2):
            window = tab_w[1][:].bitcast(U32)
            nc.vector.tensor_copy(v_w[1][:, u * HALF : (u + 1) * HALF], window.indirect(idx[:, entries(u * HALF, HALF)]))
        load_page(2, placed([P, T2], F32, "page_2", 0))
        load_page(0, placed([P, T2], F32, "page_0", 12))

        def product(jb, moving):
            acc = psum.tile([P, H], F32, name="acc", tag="bank")
            for a in range(PASSES):
                codes, scales = moving(a)
                nc.tensor.matmul_mx(
                    acc[:],
                    lhsT=v_w[a][:, jb * P : (jb + 1) * P].bitcast(FP8X4),
                    lhsT_scale=planes[:, a * ROW + jb * P : a * ROW + (jb + 1) * P],
                    rhs=codes,
                    rhs_scale=scales,
                    start=(a == 0),
                    stop=(a == PASSES - 1),
                )
            return acc[:].rearrange("j (m t) -> j t m", t=PACK)

        grouped1_1 = placed([P, H, PACK], BF16, "grouped1_1", 8)
        round_weight(1, 1, nc.vector.tensor_copy, grouped1_1[:], slice(0, SPLIT))
        round_weight(1, 1, nc.scalar.copy, grouped1_1[:], slice(SPLIT, H))

        larger = tile([P, BLOCKS, PACK, P], F32, "larger")
        for jb in range(BLOCKS):
            far = product(jb, lambda a: (w2_w[:, a, :].bitcast(FP4X4), planes[:, a * ROW + S : a * ROW + S + H]))
            nc.scalar.copy(larger[:, jb], far)

        load_page(1, tile([P, T2], F32, "page_1", over="staged_sc"))
        quantise_weight(1, 1, grouped1_1[:])
        for jb in range(BLOCKS):
            near = product(jb, lambda a: quantised[1, a])
            nc.vector.tensor_tensor(larger[:, jb], near, larger[:, jb], MAX)
        load_page(LAST, tile([P, T2], F32, "page_3", over="scales1_1"))
        w4_w = tile([P, N], I32, "w4_w", over="scales1_0")
        nc.sync.dma_start(w4_w[:], w4_words[0].rearrange("p c i -> p (c i)").bitcast(I32))

        old = {}

        def fetch_old(t, dest):
            nc.vector.tensor_copy(dest, page[t][:].indirect(idx2[:]))
            old[t] = dest

        grouped3 = tile([P, PASSES, H, PACK], BF16, "grouped3", over="w2_w")
        round_weight(3, 0, nc.scalar.copy, grouped3[:, 0])
        quantise_weight(3, 0, grouped3[:, 0], over="codes1_1")
        fetch_old(2, tile([P, S], F32, "old2", over="raw1_0")[:])
        round_weight(3, 1, nc.scalar.copy, grouped3[:, 1])
        quantise_weight(3, 1, grouped3[:, 1], over="codes1_0")
        shared = tile([P, BLOCKS, PACK, P], F32, "shared")
        for jb in range(BLOCKS):
            nc.scalar.copy(shared[:, jb], product(jb, lambda a: quantised[3, a]))
        old01 = tile([P, 2, S], F32, "old01", over="tab_w0")
        fetch_old(0, old01[:, 0, :])
        fetch_old(1, old01[:, 1, :])
        fetch_old(LAST, tile([P, S], F32, "old3", over="w2_w")[:])

        bias = tile([P, N // P], F32, "bias", over="scales3_1")
        with nc.allow_non_contiguous_dma(reason="one bias value a partition"):
            nc.sync.dma_start(bias[:], b.rearrange("(c p) -> p c", p=P))

        def features(pair):
            banks = [psum.tile([P, HALF], F32, name="h", tag="bank") for half in pair]
            for i in range(HALF // P):
                for bank, (t, u) in zip(banks, pair):
                    jb = u * (HALF // P) + i
                    for term, src in enumerate((larger, shared)):
                        nc.tensor.matmul(
                            bank[:, i * P : (i + 1) * P],
                            lhsT=src[:, jb, t, :],
                            rhs=ident[:],
                            is_transpose=True,
                            start=(term == 0),
                            stop=(term == 1),
                        )
            return banks

        def put(t, u, new):
            nc.vector.tensor_copy(page[t][:].indirect(idx2[:, entries(u * HALF, HALF)]), new[:])

        def update(pair, between=None):
            banks = features(pair)
            news = [ring.tile([P, HALF], F32, name="new", tag="new") for half in pair]
            for bank, new, (t, u) in zip(banks, news, pair):
                nc.vector.tensor_tensor(new[:], bank[:], old[t][:, u * HALF : (u + 1) * HALF], MAX)
            put(*pair[0], news[0])
            if between is not None:
                between()
            put(*pair[1], news[1])

        def fetch_read(t, dest):
            nc.vector.tensor_copy(dest, page[t][:].indirect(idx3[:]))

        x = [tile([P, PIECE, PACK], BF16, f"x{c}") for c in range(PIECES)]

        update(((2, 0), (0, 0)))
        update(((2, 1), (1, 0)))
        read2 = tile([P, M], BF16, "read2")
        fetch_read(2, read2[:])
        for c in range(PIECES):
            nc.scalar.copy(x[c][:, :, 2], read2[:, c * PIECE : (c + 1) * PIECE])
        update(((0, 1), (1, 1)))
        read01 = tile([P, 2, M], BF16, "read01", over="read2")
        fetch_read(0, read01[:, 0, :])
        update(((LAST, 0), (LAST, 1)), lambda: fetch_read(1, read01[:, 1, :]))
        for c in range(PIECES):
            nc.scalar.copy(x[c][:, :, 0:2], read01[:, :, c * PIECE : (c + 1) * PIECE].rearrange("p t m -> p m t"))

        result = tile([P, N // P, M], F32, "result", over="larger")
        out_v = out.rearrange("(n p) m -> p n m", p=P)

        def fetch_last(c):
            picked = page[LAST][:].indirect(idx3[:, entries(c * PIECE, PIECE)])
            if c < 2:
                nc.vector.tensor_copy(x[c][:, :, LAST], picked)
            else:
                value3 = tile([P, PIECE], BF16, f"value3_{c}", over=f"x{c - 2}")
                nc.vector.tensor_copy(value3[:], picked)
                nc.vector.tensor_copy(x[c][:, :, LAST], value3[:])

        def finish(c):
            codes = keep.tile([P, PIECE], U32, name=f"x_codes{c}", align_bytes=64)
            scales = keep.tile([P, PIECE], U8, name=f"x_scales{c}", align_bytes=64)
            nc.vector.quantize_mx(codes[:].bitcast(FP8X4), scales[:], x[c][:].rearrange("p m t -> p (m t)"))
            cols = slice(c * PIECE, (c + 1) * PIECE)
            for n in range(N // P):
                w4_col = n // 2 * ROW + S + H + n % 2 * P
                y = psum.tile([P, PIECE], F32, name="y", tag="bank")
                nc.tensor.matmul_mx(
                    y[:],
                    lhsT=w4_w[:, n * P : (n + 1) * P].bitcast(FP8X4),
                    lhsT_scale=planes[:, w4_col : w4_col + P],
                    rhs=codes[:].bitcast(FP8X4),
                    rhs_scale=scales[:],
                    start=True,
                    stop=True,
                )
                nc.scalar.activation(result[:, n, cols], y[:], TANH, bias=bias[:, n : n + 1])
                nc.sync.dma_start(out_v[:, n, cols], result[:, n, cols])

        for c in range(PIECES):
            fetch_last(c)
            finish(c)
